import numpy as np, ml_dtypes
CORES = [50,106,114,52,108,116]
N = 6
import mx_ref
NC, G, MB = 128, 4, 2
C = np.float32(0.041)
BF = ml_dtypes.bfloat16
def cut(t, i, w=512):
    return t[:, w * i:w * i + w]
def tile(rs):
    return np.stack(rs, axis=2).reshape(128, -1).astype(BF)
def layer(w, X):
    out = []
    for i in range(G):
        for t in range(len(X)):
            p = mx_ref.matmul(mx_ref.quantize(cut(w, len(X) * i + t)), X[t])
            z = p if t == 0 else z + p
        out.append(z)
    return out
def act(Z):
    return [np.maximum(z, 0) * C for z in Z]
def masked(U, Z):
    return [(u * (z > 0)) * C for u, z in zip(U, Z)]
def setup_inputs(rng):
    def f(*shape):
        return mx_ref.flush((rng.standard_normal(shape, dtype=np.float32) * np.exp2(rng.integers(-2, 3, shape[:-1] + (1,)))).astype(BF))
    return {"x": f(N, 128, MB * 4 * NC), "e": f(N, 128, MB * 4 * NC), "w": f(N, 128, G * 512), "v": f(N, 128, G * 512)}
def setup_inputs_blocks(rng):
    d = setup_inputs(rng)
    for k in ("x", "e"): d[k] = mx_ref.spread(d[k], rng, 4)
    for k in ("w", "v"): d[k] = mx_ref.spread(d[k], rng, 1)
    return d
def setup_inputs_wide(rng):
    d = setup_inputs(rng)
    for k in ("x", "e"): d[k] = mx_ref.flush((d[k].astype(np.float32) * np.exp2(rng.integers(-8, 9, (N, 1, 1))).astype(np.float32)).astype(BF))
    return d
def setup_inputs_zeros(rng):
    d = setup_inputs(rng); v = d["x"].reshape(N, 128, -1, 4).copy()
    v[np.broadcast_to((rng.random((N, 1, v.shape[2], 1)) < 0.33), v.shape)] = 0
    d["x"] = v.reshape(d["x"].shape)
    return d
def reference(x, e, w, v):
    y = np.full((N, 128, MB * G * NC), np.nan, np.float32)
    for m in range(MB):
        a = mx_ref.quantize(cut(x[N - 1], m, 4 * NC)); Z = []
        for s in range(N):
            Z.append(layer(w[s], [a]))
            if s < N - 1: a = mx_ref.quantize(tile(act(Z[s])))
        b = mx_ref.quantize(cut(e[0], m, 4 * NC))
        for s in range(N - 1, 0, -1):
            b = mx_ref.quantize(tile(masked(layer(v[s], [b]), Z[s])))
        U = layer(v[0], [b])
        for i in range(G):
            y[0][:, NC * (G * m + i):NC * (G * m + i) + NC] = U[i] * (Z[0][i] > 0)
    return {"y": y}

from concourse.bass import DstId, RemoteDMATransfer
from concourse.mybir import dt, AluOpType, ActivationFunctionType

C = 0.041
W = 128
MB = 2
G = 4
X4 = "float8_e4m3fn_x4"
SCRATCH = {
    "xt": ("sbuf", [128, 1024], "bfloat16"),
    "wt": ("sbuf", [128, 2048], "bfloat16"),
    "vt": ("sbuf", [128, 2048], "bfloat16"),
    "wc": ("sbuf", [128, 512], X4), "wsc": ("sbuf", [128, 512], "uint8"),
    "vc": ("sbuf", [128, 512], X4), "vsc": ("sbuf", [128, 512], "uint8"),
    "ac": ("sbuf", [128, 256], X4), "asc": ("sbuf", [128, 256], "uint8"),
    "bc": ("sbuf", [128, 256], X4), "bsc": ("sbuf", [128, 256], "uint8"),
    "ec": ("sbuf", [128, 256], X4), "esc": ("sbuf", [128, 256], "uint8"),
    "oc": ("sbuf", [128, 512], X4), "osc": ("sbuf", [128, 512], "uint8"),
    "h": ("sbuf", [128, 2048], "bfloat16"),
    "mk": ("sbuf", [128, 1024], "float32"),
    "sgn": ("sbuf", [128, 256], "float32"),
    "yt": ("sbuf", [128, 1024], "float32"),
    "ps": ("psum", [128, 4096], "float32"),
}
SEMAPHORES = (["lw", "lv", "lx0", "lx1", "qw", "qv", "qx0", "qx1", "ep", "ea", "sent", "first", "yd", "ye"]
              + [n + str(m) for m in range(MB) for n in
                 ("a", "b", "ac", "as", "bc", "bs", "rv", "rs", "q", "m", "sg", "sm", "bv", "qb", "y")]
              + [n + "%d_%d" % (m, b) for m in range(MB) for b in range(G) for n in ("z", "u")])


def bits(mask):
    return [1 << k for k in range(mask.bit_length()) if mask >> k & 1]


def relay(T, topo, src, dst):
    if topo.may_write(src, dst):
        return None
    for c in range(topo.CHIPS * topo.CORES_PER_CHIP):
        if topo.chip(c) == topo.chip(src) and topo.die(c) == topo.die(src) and T.rank_of(c) is None \
                and topo.may_write(c, dst):
            return c


def rank_program(g, core, T, topo):
    R = list(T.cores)
    N = len(R)
    last = N - 1
    rank = T.rank_of(core)
    sem = T.sem
    sent = {"sent": 0, "first": 0}

    def count(mask):
        return len(bits(mask))

    def send(dst, out, in_, rsem, local="sent", mask=None):
        mask = topo.mask(core, dst) if mask is None else mask
        rid, pid = topo.addr(dst)[:2]
        g.remote_dma(out, in_, sem[rsem], sem[local], pid, rid, mask)
        sent[local] += count(mask)

    def codes(buf, lo, n):
        return buf[:, lo:lo + n].bitcast(dt.uint8)

    hop = {"a": {s: s + 1 for s in range(N - 1)}, "b": {s: s - 1 for s in range(1, N)}}
    rel = {(d, s): relay(T, topo, R[s], R[hop[d][s]]) for d in hop for s in hop[d]}
    land = {"a": (T.ac, T.asc), "b": (T.bc, T.bsc)}

    def forward(d, s, m, lo):
        lc, ls = land[d]
        r = rel[d, s]
        dst = R[hop[d][s]] if r is None else r
        k = "%d" % m
        send(dst, codes(lc, W * m, W), codes(T.oc, lo, W), d + k if r is None else d + "c" + k)
        send(dst, ls[:, W * m:W * m + W], T.osc[:, lo:lo + W], d + k if r is None else d + "s" + k)

    stops = [R[1], R[2], R[3], R[4], rel["b", last]]
    via = {k: rel["a", k + 1] for k in range(4) if rel["a", k + 1] is not None}
    P = 64

    def piece(cb, sb, k, base=0):
        return codes(cb, base + P * k, P) if k < 4 else sb[:, base:base + 2 * W]

    def pass_piece(k, came, dst, rsem, mask):
        g.wait_ge(sem.ep, came)
        send(dst, piece(T.ec, T.esc, k), piece(T.ec, T.esc, k), rsem, mask=mask)

    off = bits(topo.mask(R[0], R[1]))
    here = [b for b in bits(topo.mask(R[0], R[3])) if b not in off]
    masks = []
    for k, c in enumerate(stops):
        if topo.chip(c) == topo.chip(R[0]):
            masks.append(sum(here[0:2]))
        else:
            j = sum(1 for q in stops[:k] if topo.chip(q) != topo.chip(R[0]))
            masks.append(sum(off[2 * j:2 * j + 2]))

    if rank is None:
        jobs = [(d, s) for d in ("a", "b") for s in sorted(hop[d]) if rel[d, s] == core]
        if not jobs:
            return
        for k in range(5):
            if stops[k] == core or via.get(k) == core:
                came = count(masks[k]) if stops[k] == core else count(topo.mask(stops[k], core))
                pass_piece(k, came, R[last], "ea", topo.mask(core, R[hop[jobs[0][0]][jobs[0][1]]]))
        for d, s in jobs:
            lc, ls = land[d]
            dst = R[hop[d][s]]
            came = count(topo.mask(R[s], core))
            for m in range(MB):
                k = "%d" % m
                g.wait_ge(sem[d + "c" + k], came)
                send(dst, codes(lc, W * m, W), codes(lc, W * m, W), d + k)
                g.wait_ge(sem[d + "s" + k], came)
                send(dst, ls[:, W * m:W * m + W], ls[:, W * m:W * m + W], d + k)
        g.wait_ge(sem.sent, sent["sent"])
        return

    v, t, s_, sy = g.vector, g.tensor, g.scalar, g.sync

    def bank(k, lo=0, n=W):
        return T.ps[:, 512 * k + lo:512 * k + lo + n]

    def hcols(slot, b):
        return T.h[:, 512 * slot + b:512 * slot + 512:4]

    def mask_ap(m, b):
        return T.mk[:, 512 * m + W * b:512 * m + W * b + W]

    def arrival(d, m):
        if d == "a" and rank == 0:
            src = R[last]
        else:
            s = rank - 1 if d == "a" else rank + 1
            src = R[s] if rel[d, s] is None else rel[d, s]
        return 2 * count(topo.mask(src, core))

    def quant(cout, sout, in_, done):
        v.quantize_mx(cout, sout, in_).then_inc(sem[done], 1)

    def quant_w():
        v.wait_ge(sem.lw, 16)
        quant(T.wc[:, 0:512], T.wsc[:, 0:512], T.wt[:, 0:2048], "qw")

    def quant_v():
        v.wait_ge(sem.lv, 16)
        quant(T.vc[:, 0:512], T.vsc[:, 0:512], T.vt[:, 0:2048], "qv")

    def load_w():
        sy.dma_start(T.wt[:, 0:2048], T.w[:, 0:2048]).then_inc(sem.lw, 16)

    def load_v():
        sy.dma_start(T.vt[:, 0:2048], T.v[:, 0:2048]).then_inc(sem.lv, 16)

    def products(wc, ws, xc, xs, lo, n, base, name):
        for b in range(G):
            t.matmul_mx(bank(base + b, 0, n), wc[:, W * b:W * b + W], ws[:, W * b:W * b + W],
                        xc[:, lo:lo + n], xs[:, lo:lo + n], True, True).then_inc(sem[name + "_%d" % b], 1)

    if rank == last:
        for m in range(MB):
            sy.dma_start(T.xt[:, 512 * m:512 * m + 512], T.x[:, 512 * m:512 * m + 512]).then_inc(sem["lx%d" % m], 16)
    elif rank == 0:
        sy.dma_start(T.xt[:, 0:1024], T.e[:, 0:1024]).then_inc(sem.lx0, 16)
        load_w()
    else:
        load_w()
        load_v()

    if rank == last:
        for m in range(MB):
            v.wait_ge(sem["lx%d" % m], 16)
            quant(T.oc[:, W * m:W * m + W], T.osc[:, W * m:W * m + W], T.xt[:, 512 * m:512 * m + 512], "qx%d" % m)
            g.wait_ge(sem["qx%d" % m], 1)
            send(R[0], codes(T.ac, W * m, W), codes(T.oc, W * m, W), "a%d" % m, "first")
            send(R[0], T.asc[:, W * m:W * m + W], T.osc[:, W * m:W * m + W], "a%d" % m, "first")
        sy.wait_ge(sem.first, sent["first"])
        load_v()
        load_w()
        quant_v()
        quant_w()
        came = 0
        for k in range(5):
            src = via.get(k, stops[k])
            if T.rank_of(src) is not None:
                dst = R[hop["a"][T.rank_of(src)]]
            else:
                dst = [R[hop[d][s]] for d in ("a", "b") for s in sorted(hop[d]) if rel[d, s] == src][0]
            came += count(topo.mask(src, dst))
        t.wait_ge(sem.qv, 1)
        t.wait_ge(sem.ea, came)
        products(T.vc, T.vsc, T.ec, T.esc, 0, MB * W, 4, "u0")
        t.wait_ge(sem.qw, 1)
        for m in range(MB):
            k = "%d" % m
            t.wait_ge(sem["a" + k], arrival("a", m))
            if m:
                t.wait_ge(sem["m%d" % (m - 1)], G - 1)
                t.wait_ge(sem["sg%d" % (m - 1)], 1)
            products(T.wc, T.wsc, T.ac, T.asc, W * m, W, 0, "z" + k)
            s_.wait_ge(sem["z%s_1" % k], 1)
            s_.activation(T.sgn[:, W * m:W * m + W], bank(1), ActivationFunctionType.Sign).then_inc(sem["sg" + k], 1)
            s_.wait_ge(sem["sg" + k], 1)
            s_.activation(mask_ap(m, 1), T.sgn[:, W * m:W * m + W], ActivationFunctionType.Relu,
                          scale=C).then_inc(sem["sm" + k], 1)
            done = 0
            for b in (0, 2, 3, 1):
                if b == 1:
                    v.wait_ge(sem["sm" + k], 1)
                else:
                    done += 1
                    v.wait_ge(sem["z%s_%d" % (k, b)], 1)
                    v.tensor_scalar(mask_ap(m, b), bank(b), 0.0, C, AluOpType.is_gt, AluOpType.mult).then_inc(sem["m" + k], 1)
                    v.wait_ge(sem["m" + k], done)
                if m == 0:
                    v.wait_ge(sem["u0_%d" % b], 1)
                v.tensor_tensor(hcols(2 + m, b), bank(4 + b, W * m), mask_ap(m, b), AluOpType.mult).then_inc(sem["bv" + k], 1)
            v.wait_ge(sem["bv" + k], G)
            lo = W * (2 + m)
            quant(T.oc[:, lo:lo + W], T.osc[:, lo:lo + W], T.h[:, 512 * (2 + m):512 * (3 + m)], "qb" + k)
            g.wait_ge(sem["qb" + k], 1)
            forward("b", rank, m, lo)
        g.wait_ge(sem.sent, sent["sent"])
        return

    if rank == 0:
        v.wait_ge(sem.lx0, 16)
        quant(T.oc[:, 2 * W:4 * W], T.osc[:, 2 * W:4 * W], T.xt[:, 0:1024], "qx0")
        g.wait_ge(sem.qx0, 1)
        tr = []
        for k, c in enumerate(stops):
            rid, pid = topo.addr(c)[:2]
            tr.append(RemoteDMATransfer(dst_ids=[DstId(rid=rid, pnc=pid)], dma_engine_mask=masks[k], remote_sem=sem.ep,
                                        src=piece(T.oc, T.osc, k, 2 * W), dst=piece(T.ec, T.esc, k)))
            sent["first"] += count(masks[k])
        g.remote_dma_fused(tr, local_sem=sem.first)
    else:
        k = rank - 1
        if k in via:
            pass_piece(k, count(masks[k]), via[k], "ep", topo.mask(core, via[k]))
        else:
            pass_piece(k, count(masks[k]), R[last], "ea", topo.mask(core, R[hop["a"][rank]]))
    quant_w()
    if rank > 1:
        quant_v()

    t.wait_ge(sem.qw, 1)
    for m in range(MB):
        k = "%d" % m
        t.wait_ge(sem["a" + k], arrival("a", m))
        products(T.wc, T.wsc, T.ac, T.asc, W * m, W, 4 * m, "z" + k)
        s_.wait_ge(sem["z%s_1" % k], 1)
        s_.activation(hcols(m, 1), bank(4 * m + 1), ActivationFunctionType.Relu, scale=C).then_inc(sem["rs" + k], 1)
        for b in (0, 2, 3):
            v.wait_ge(sem["z%s_%d" % (k, b)], 1)
            v.tensor_scalar(hcols(m, b), bank(4 * m + b), 0.0, C, AluOpType.max, AluOpType.mult).then_inc(sem["rv" + k], 1)
        v.wait_ge(sem["rs" + k], 1)
        v.wait_ge(sem["rv" + k], G - 1)
        quant(T.oc[:, W * m:W * m + W], T.osc[:, W * m:W * m + W], T.h[:, 512 * m:512 * m + 512], "q" + k)
        for b in range(G):
            if rank == 0:
                v.tensor_scalar(mask_ap(m, b), bank(4 * m + b), 0.0, None, AluOpType.is_gt).then_inc(sem["m" + k], 1)
            else:
                v.tensor_scalar(mask_ap(m, b), bank(4 * m + b), 0.0, C, AluOpType.is_gt, AluOpType.mult).then_inc(sem["m" + k], 1)
        g.wait_ge(sem["q" + k], 1)
        forward("a", rank, m, W * m)

    if rank == 0:
        sy.wait_ge(sem.first, sent["first"])
        sy.wait_ge(sem.sent, sent["sent"])
        load_v()
    if rank <= 1:
        quant_v()

    t.wait_ge(sem.qv, 1)
    for m in range(MB):
        k = "%d" % m
        t.wait_ge(sem["m" + k], G)
        t.wait_ge(sem["b" + k], arrival("b", m))
        products(T.vc, T.vsc, T.bc, T.bsc, W * m, W, 4 * m, "u" + k)
        v.wait_ge(sem["m" + k], G)
        for b in range(G):
            v.wait_ge(sem["u%s_%d" % (k, b)], 1)
            if rank == 0:
                blk = 512 * m + W * b
                v.tensor_tensor(T.yt[:, blk:blk + W], bank(4 * m + b), mask_ap(m, b), AluOpType.mult).then_inc(
                    sem[("bv" if b < 2 else "y") + k], 1)
            else:
                v.tensor_tensor(hcols(2 + m, b), bank(4 * m + b), mask_ap(m, b), AluOpType.mult).then_inc(sem["bv" + k], 1)
        if rank == 0:
            for q, w, d, lo in ((sy, "bv", "yd", 512 * m), (s_, "y", "ye", 512 * m + 256)):
                q.wait_ge(sem[w + k], 2)
                q.dma_start(T.y[:, lo:lo + 256], T.yt[:, lo:lo + 256]).then_inc(sem[d], 16)
        else:
            v.wait_ge(sem["bv" + k], G)
            lo = W * (2 + m)
            quant(T.oc[:, lo:lo + W], T.osc[:, lo:lo + W], T.h[:, 512 * (2 + m):512 * (3 + m)], "qb" + k)
            g.wait_ge(sem["qb" + k], 1)
            forward("b", rank, m, lo)
    if rank == 0:
        sy.wait_ge(sem.yd, 16 * MB)
        s_.wait_ge(sem.ye, 16 * MB)
    g.wait_ge(sem.sent, sent["sent"])
